import numpy as np
import ml_dtypes


def mxq(x, axis, fmt="e4m3"):
    dtype, down = {"e4m3": (ml_dtypes.float8_e4m3fn, 7), "e5m2": (ml_dtypes.float8_e5m2, 14)}[fmt]
    v = np.moveaxis(np.asarray(x, np.float32).astype(ml_dtypes.bfloat16).astype(np.float64), axis, -1)
    blocks = v.reshape(v.shape[:-1] + (-1, 32))
    amax = np.abs(blocks).max(-1, keepdims=True)
    byte = np.maximum(np.where(amax > 0, np.frexp(amax)[1] - 1 + 127, 0) - down, 1)
    scale = np.exp2(byte - 127.0)
    codes = (blocks / scale).astype(np.float32).astype(dtype).astype(np.float64)
    return np.moveaxis((codes * scale).reshape(v.shape), -1, axis)


WIDE = False


def mx_kscale(k):
    if not WIDE:
        return np.ones(k)
    levels = np.array([10, -10, 5, -5, 0])
    if k % 512:
        return np.exp2(np.random.permutation(np.resize(levels, k // 32))).repeat(32)
    a = np.empty((k // 512, 16))
    for p in range(k // 512):
        a[p, :8] = np.random.permutation(np.resize(levels, 8))
        for g in range(8):
            far = levels[np.abs(levels - a[p, g]) >= 10]
            a[p, g + 8] = far[np.random.randint(len(far))]
    return np.exp2(a.ravel()).repeat(32)


def f64(x):
    return np.asarray(x).astype(np.float64)


def striped(idx):
    return np.tile(idx.reshape(-1, 16).T, (8, 1)).astype(np.uint16)


def unstriped(offs):
    return offs[:16].T.reshape(-1).astype(np.int64)


E2M1 = np.array([0.0, 0.5, 1.0, 1.5, 2.0, 3.0, 4.0, 6.0, -0.0, -0.5, -1.0, -1.5, -2.0, -3.0, -4.0, -6.0])


def pack_weight(w, fmt):
    k, n = w.shape
    w = f64(np.asarray(w, np.float32).astype(ml_dtypes.bfloat16)).reshape(k // 32, 32, n)
    amax = np.abs(w).max(1)
    if fmt == "e4m3":
        byte = np.frexp(amax)[1] - 1 + 127 - 7
    else:
        mant, ex = np.frexp(amax / 6.0)
        byte = np.where(mant > 0.5, ex, ex - 1) + 127
    byte = np.clip(np.where(amax > 0, byte, 1), 1, 254)
    scaled = (w * np.exp2(127.0 - byte)[:, None, :]).reshape(k, n).astype(np.float32)
    by_word = np.ascontiguousarray(scaled.reshape(k // 512, 128, 4, n).transpose(0, 1, 3, 2))
    if fmt == "e4m3":
        words = by_word.astype(ml_dtypes.float8_e4m3fn).view(np.uint8)
    else:
        c = by_word.astype(ml_dtypes.float4_e2m1fn).view(np.uint8) & 0xF
        words = (c[..., 0::2] | (c[..., 1::2] << 4)).reshape(k // 512, 128, 2 * n)
    return np.ascontiguousarray(words), np.ascontiguousarray(byte.astype(np.uint8).reshape(k // 512, 16, n))


def unpack_weight(words, scales, fmt):
    g, _, n = scales.shape
    words = np.ascontiguousarray(words).reshape(g, 128, n, -1)
    if fmt == "e4m3":
        vals = words.view(ml_dtypes.float8_e4m3fn).astype(np.float64)
    else:
        nib = np.empty((g, 128, n, 4), np.uint8)
        nib[..., 0::2] = words & 0xF
        nib[..., 1::2] = words >> 4
        vals = E2M1[nib]
    vals = vals * np.repeat(np.exp2(scales.astype(np.float64) - 127.0), 8, axis=1)[..., None]
    return vals.transpose(0, 1, 3, 2).reshape(g * 512, n)


def gelu(v):
    return 0.5 * v * (1.0 + np.tanh(np.sqrt(2.0 / np.pi) * (v + 0.044715 * v**3)))


def bf(x):
    return np.asarray(x, np.float32).astype(ml_dtypes.bfloat16)


def planes(Y):
    n, m = Y.shape
    b = f64(bf(Y)).reshape(n // 32, 32, m)
    amax = np.abs(b).max(1)
    byte = np.clip(np.where(amax > 0, np.frexp(amax)[1] - 1 + 127 - 7, 1), 1, 254)
    codes = (b * np.exp2(127.0 - byte)[:, None, :]).reshape(n, m).astype(np.float32).astype(ml_dtypes.float8_e4m3fn).view(np.uint8)
    words = codes.reshape(n // 512, 128, 4, m).transpose(0, 1, 3, 2)
    return np.ascontiguousarray(words), np.ascontiguousarray(byte.astype(np.uint8).reshape(n // 512, 16, m))


K, H, N, T, S, P = 1024, 512, 1024, 2048, 1024, 512

def setup_inputs():
    n = np.random.standard_normal
    s = mx_kscale(K)[:, None]
    u = mx_kscale(H)[:, None]
    tab_words, tab_scales = pack_weight(n((K, T)) * s, "e4m3")
    wa_words, wa_scales = pack_weight(0.55 * n((H, N)) / np.sqrt(H) / u, "e2m1")
    return {
        "tab_words": tab_words, "tab_scales": tab_scales,
        "offs": striped(np.random.permutation(T)[:S]),
        "pos1": striped(np.random.permutation(S)[:P]),
        "pos2": striped(np.random.permutation(S)[:P]),
        "w1": (n((K, H)) / np.sqrt(K) / s * u.T).astype(np.float32),
        "b1": (0.5 * n(H) * u[:, 0]).astype(np.float32),
        "wa_words": wa_words, "wa_scales": wa_scales,
        "res": (0.5 * n((N, S))).astype(np.float32),
        "wb": (0.8 * n((H, N)) / np.sqrt(H) / u).astype(np.float32),
        "steep": np.random.uniform(1, 3, N).astype(np.float32),
        "share": np.random.uniform(0.1, 0.5, N).astype(np.float32),
        "ref": (0.7 * n(N)).astype(np.float32),
        "gain": (1.5 * np.exp(0.8 * n(N))).astype(np.float32),
    }

def reference(tab_words, tab_scales, offs, pos1, pos2, w1, b1, wa_words, wa_scales, res, wb, steep, share, ref, gain):
    v = unpack_weight(tab_words, tab_scales, "e4m3")[:, unstriped(offs)]
    wa = unpack_weight(wa_words, wa_scales, "e2m1")
    h = (mxq(f64(w1), 0, "e4m3").T @ v) + f64(b1)[:, None]
    hq = mxq(h, 0, "e4m3")
    e = (wa.T @ hq) + f64(res)
    d = mxq(f64(wb), 0, "e4m3").T @ hq
    top = e.max(axis=1)
    a = 1.0 / (1.0 + np.exp(-f64(steep)[:, None] * (e[:, unstriped(pos1)] - f64(share)[:, None] * top[:, None])))
    c = d[:, unstriped(pos2)] - f64(ref)[:, None]
    y = f64(gain)[:, None] * (c * a)
    words, scales = planes(y)
    return y, words, scales

@@ -1,0 +1,242 @@
+from contextlib import ExitStack
+
+import concourse.mybir as mybir
+
+F32 = mybir.dt.float32
+BF16 = mybir.dt.bfloat16
+I32 = mybir.dt.int32
+U32 = mybir.dt.uint32
+U16 = mybir.dt.uint16
+U8 = mybir.dt.uint8
+FP8X4 = mybir.dt.float8_e4m3fn_x4
+FP4X4 = mybir.dt.float4_e2m1fn_x4
+ALU = mybir.AluOpType
+ACT = mybir.ActivationFunctionType
+AXIS = mybir.AxisListType
+
+K, H, N, T, S, M = 1024, 512, 1024, 2048, 1024, 512
+P = 128
+FLOPS = 2 * K * H * S + 2 * 2 * H * N * S
+
+
+def tile_list_clock_selector_scores_kernel(
+    tc, tab_words, tab_scales, offs, pos1, pos2, w1, b1, wa_words, wa_scales, res, wb, steep, share, ref, gain,
+    out_0, out_1, out_2,
+):
+    nc = tc.nc
+    with ExitStack() as ctx:
+        lists = ctx.enter_context(tc.tile_pool(name="lists", bufs=1))
+        keep = ctx.enter_context(tc.tile_pool(name="keep", bufs=1))
+        ring = ctx.enter_context(tc.tile_pool(name="ring", bufs=3))
+        psum = ctx.enter_context(tc.psum_pool(name="psum", bufs=1))
+
+        def held(name, shape, dtype):
+            return keep.tile(shape, dtype, name=name, align_bytes=64)
+
+        def bank(b, name):
+            return psum.tile([P, 512], F32, name=name, tag="bank%d" % b)
+
+        offs_t = lists.tile([P, S // 16], U16, name="offs_t")
+        pos1_t = lists.tile([P, M // 16], U16, name="pos1_t")
+        pos2_t = lists.tile([P, M // 16], U16, name="pos2_t")
+
+        tab_w = [held("tab_w%d" % a, [P, T], I32) for a in range(2)]
+        tab_s = held("tab_s", [P, T], U8)
+        wa_w = held("wa_w", [P, 2 * N], U8)
+        wa_s = held("wa_s", [P, N], U8)
+        w1_lo = held("w1_lo", [P, 4, H], F32)
+        w1_hi = [held("w1_hi%d" % c, [P, 4, H // 2], F32) for c in range(2)]
+        wb_raw = [held("wb_raw%d" % g, [P, 4, 512], F32) for g in range(2)]
+        res_t = [held("res%d" % i, [P, S], F32) for i in range(8)]
+        b1_t = held("b1_t", [P, 4], F32)
+        steep_t = held("steep_t", [P, 8], F32)
+        share_t = held("share_t", [P, 8], F32)
+        ref_t = held("ref_t", [P, 8], F32)
+        gain_t = held("gain_t", [P, 8], F32)
+
+        nc.vector.memset(tab_s[:].bitcast(I32), 0)
+        nc.vector.memset(wa_s[:].bitcast(I32), 0)
+
+        def load_words(a):
+            nc.sync.dma_start(out=tab_w[a][:], in_=tab_words[a].rearrange("p t i -> p (t i)").bitcast(I32))
+
+        def load_rows(tile, vec):
+            nc.sync.dma_start(out=tile[:].rearrange("p (g t) -> p g t", t=4), in_=vec.rearrange("(g p t) -> p g t", g=2, t=4))
+
+        res_v = res.rearrange("(g p t) j -> g t p j", g=2, t=4)
+        out_v = out_0.rearrange("(g p t) m -> g t p m", g=2, t=4)
+        w1_v = w1.rearrange("(a p j) c -> a p j c", a=2, j=4)
+        wb_v = wb.rearrange("(p j) c -> p j c", j=4)
+
+        nc.sync.dma_start(offs_t[:], offs)
+        nc.sync.dma_start(out=w1_lo[:], in_=w1_v[0])
+        for q in range(4):
+            nc.sync.dma_start(out=tab_s[32 * q : 32 * q + 8, :].bitcast(I32), in_=tab_scales[:, 4 * q : 4 * q + 4, :].bitcast(I32))
+        load_words(0)
+        load_words(1)
+        nc.sync.dma_start(out=b1_t[:], in_=b1.rearrange("(p t) -> p t", t=4))
+        for c in range(2):
+            nc.sync.dma_start(out=w1_hi[c][:], in_=w1_v[1][:, :, 256 * c : 256 * (c + 1)])
+        for q in range(4):
+            nc.gpsimd.dma_start(out=wa_s[32 * q : 32 * q + 4, :].bitcast(I32), in_=wa_scales[0, 4 * q : 4 * q + 4, :].bitcast(I32))
+        nc.sync.dma_start(out=wa_w[:].bitcast(I32), in_=wa_words[0].bitcast(I32))
+        nc.sync.dma_start(out=wb_raw[0][:], in_=wb_v[:, :, 0:512])
+        load_rows(steep_t, steep)
+        load_rows(share_t, share)
+        nc.sync.dma_start(out=res_t[0][:], in_=res_v[0, 0])
+        nc.sync.dma_start(pos1_t[:], pos1)
+        nc.sync.dma_start(pos2_t[:], pos2)
+        nc.sync.dma_start(out=res_t[1][:], in_=res_v[0, 1])
+        load_rows(ref_t, ref)
+        load_rows(gain_t, gain)
+        nc.sync.dma_start(out=res_t[2][:], in_=res_v[0, 2])
+        nc.sync.dma_start(out=wb_raw[1][:], in_=wb_v[:, :, 512:1024])
+        for i in range(3, 8):
+            nc.sync.dma_start(out=res_t[i][:], in_=res_v[i // 4, i % 4])
+
+        def deal(copy, dst, src, m0, m1, src_m0):
+            d = dst[:].rearrange("p (t m j) -> p m j t", t=4, j=4)[:, m0:m1]
+            s = src[:].rearrange("p j (m t) -> p m j t", t=4)[:, m0 - src_m0 : m1 - src_m0]
+            copy(out=d, in_=s)
+
+        def quantize(name, src):
+            codes = held(name + "_c", [P, 512], U32)
+            scales = held(name + "_s", [P, 512], U8)
+            nc.vector.quantize_mx(out=codes[:].bitcast(FP8X4), scales=scales[:], in_=src[:])
+            return codes, scales
+
+        w1_bf = [held("w1_bf%d" % a, [P, 2048], BF16) for a in range(2)]
+        v_w = [held("v_w%d" % a, [P, S], U32) for a in range(2)]
+        v_s = held("v_s", [P, S], U8)
+
+        deal(nc.scalar.copy, w1_bf[0], w1_lo, 0, 128, 0)
+        nc.vector.tensor_copy(out=v_s[:], in_=tab_s[:].indirect(offs_t[:]))
+        nc.vector.tensor_copy(out=v_w[0][:], in_=tab_w[0][:].bitcast(U32).indirect(offs_t[:]))
+        w1_q = [quantize("w1q0", w1_bf[0])]
+        h_ps = [bank(b, "h_ps%d" % b) for b in range(8)]
+
+        def first_pass(a, b):
+            cols = slice(128 * b, 128 * (b + 1))
+            for t in range(4):
+                ts = slice(128 * t, 128 * (t + 1))
+                nc.tensor.matmul_mx(
+                    out=h_ps[b][:, ts],
+                    lhsT=w1_q[a][0][:, ts].bitcast(FP8X4),
+                    lhsT_scale=w1_q[a][1][:, ts],
+                    rhs=v_w[a][:, cols].bitcast(FP8X4),
+                    rhs_scale=v_s[4 * a : P, cols],
+                    start=(a == 0 and t == 0),
+                    stop=(a == 1 and t == 3),
+                )
+
+        for b in range(8):
+            first_pass(0, b)
+        nc.vector.tensor_copy(out=v_w[1][:], in_=tab_w[1][:].bitcast(U32).indirect(offs_t[:]))
+        deal(nc.scalar.copy, w1_bf[1], w1_hi[0], 0, 64, 0)
+        deal(nc.scalar.copy, w1_bf[1], w1_hi[1], 64, 96, 64)
+        deal(nc.vector.tensor_copy, w1_bf[1], w1_hi[1], 96, 128, 64)
+        w1_q.append(quantize("w1q1", w1_bf[1]))
+        for b in range(8):
+            first_pass(1, b)
+
+        wa_wd = [held("wa_wd%d" % g, [P, 1024], U8) for g in range(2)]
+        wa_sd = [held("wa_sd%d" % g, [P, 512], U8) for g in range(2)]
+        for g in range(2):
+            nc.gpsimd.tensor_copy(
+                out=wa_wd[g][:].rearrange("p (t m b) -> p t m b", t=4, b=2),
+                in_=wa_w[:, 1024 * g : 1024 * (g + 1)].rearrange("p (m t b) -> p t m b", t=4, b=2),
+            )
+            nc.gpsimd.tensor_copy(
+                out=wa_sd[g][:].rearrange("p (t m) -> p t m", t=4),
+                in_=wa_s[:, 512 * g : 512 * (g + 1)].rearrange("p (m t) -> p t m", t=4),
+            )
+
+        wb_bf = [held("wb_bf%d" % g, [P, 2048], BF16) for g in range(2)]
+        deal(nc.scalar.copy, wb_bf[0], wb_raw[0], 0, 128, 0)
+
+        h_bf = [held("h_bf%d" % u, [P, 2048], BF16) for u in range(2)]
+        b1_b = b1_t[:].unsqueeze(1).to_broadcast([P, 128, 4])
+        h_q = []
+        for b in range(8):
+            nc.vector.tensor_tensor(
+                out=h_bf[b // 4][:, 512 * (b % 4) : 512 * (b % 4 + 1)].rearrange("p (n t) -> p n t", t=4),
+                in0=h_ps[b][:].rearrange("p (t n) -> p n t", t=4),
+                in1=b1_b,
+                op=ALU.add,
+            )
+            if b == 4:
+                h_q.append(quantize("hq0", h_bf[0]))
+        neg_ss = held("neg_ss", [P, 8], F32)
+        neg_ref = held("neg_ref", [P, 8], F32)
+        nc.vector.scalar_tensor_tensor(out=neg_ss[:], in0=steep_t[:], scalar=-1.0, in1=share_t[:], op0=ALU.mult, op1=ALU.mult)
+        h_q.append(quantize("hq1", h_bf[1]))
+        nc.vector.tensor_scalar(out=neg_ref[:], in0=ref_t[:], scalar1=-1.0, scalar2=None, op0=ALU.mult)
+        wb_q = [quantize("wbq0", wb_bf[0])]
+
+        top = held("top", [P, 8], F32)
+        gate_b = held("gate_b", [P, 8], F32)
+        y = [held("y%d" % g, [P, 4, M], F32) for g in range(2)]
+        y_bf = [held("y_bf%d" % g, [P, 2048], BF16) for g in range(2)]
+
+        def weave(copy, g, c0, c1):
+            d = y_bf[g][:].rearrange("p (c i t) -> p c t i", i=4, t=4)[:, c0:c1]
+            s = y[g][:].rearrange("p t (c i) -> p c t i", i=4)[:, c0:c1]
+            copy(out=d, in_=s)
+
+        def planes(g):
+            codes, scales = quantize("yq%d" % g, y_bf[g])
+            nc.sync.dma_start(out=out_1[g].rearrange("p m t -> p (m t)").bitcast(I32), in_=codes[:].bitcast(I32))
+            for q in range(4):
+                queue = nc.scalar if (g == 1 and q % 2 == 1) else nc.sync
+                queue.dma_start(out=out_2[g, 4 * q : 4 * q + 4, :].bitcast(I32), in_=scales[32 * q : 32 * q + 4, :].bitcast(I32))
+
+        for i in range(8):
+            g, t = i // 4, i % 4
+            ts = slice(128 * t, 128 * (t + 1))
+            col = slice(i, i + 1)
+            e_ps = [bank(4 * (i % 2) + u, "e_ps%d_%d" % (i, u)) for u in range(2)]
+            d_ps = [bank(4 * (i % 2) + 2 + u, "d_ps%d_%d" % (i, u)) for u in range(2)]
+            for u in range(2):
+                nc.tensor.matmul_mx(
+                    out=e_ps[u][:], lhsT=wa_wd[g][:, 256 * t : 256 * (t + 1)].bitcast(FP4X4), lhsT_scale=wa_sd[g][:, ts],
+                    rhs=h_q[u][0][:].bitcast(FP8X4), rhs_scale=h_q[u][1][:], start=True, stop=True,
+                )
+            for u in range(2):
+                nc.tensor.matmul_mx(
+                    out=d_ps[u][:], lhsT=wb_q[g][0][:, ts].bitcast(FP8X4), lhsT_scale=wb_q[g][1][:, ts],
+                    rhs=h_q[u][0][:].bitcast(FP8X4), rhs_scale=h_q[u][1][:], start=True, stop=True,
+                )
+            e = ring.tile([P, S], F32, name="e")
+            d = ring.tile([P, S], F32, name="d")
+            a = ring.tile([P, M], F32, name="a")
+            c = ring.tile([P, M], F32, name="c")
+            cg = ring.tile([P, M], F32, name="cg")
+            for u in range(2):
+                js = slice(512 * u, 512 * (u + 1))
+                nc.vector.tensor_tensor(out=e[:, js], in0=e_ps[u][:], in1=res_t[i][:, js], op=ALU.add)
+            for u in range(2):
+                nc.scalar.copy(out=d[:, 512 * u : 512 * (u + 1)], in_=d_ps[u][:])
+            nc.vector.tensor_reduce(out=top[:, col], in_=e[:], axis=AXIS.X, op=ALU.max)
+            if i == 0:
+                nc.vector.tensor_scalar(out=gate_b[:, col], in0=top[:, col], scalar1=neg_ss[:, col], scalar2=None, op0=ALU.mult)
+            else:
+                nc.scalar.activation(out=gate_b[:, col], in_=top[:, col], func=ACT.Identity, scale=neg_ss[:, col])
+            nc.scalar.activation(
+                out=a[:], in_=e[:].indirect(pos1_t[:]), func=ACT.Sigmoid, bias=gate_b[:, col], scale=steep_t[:, col]
+            )
+            nc.vector.tensor_copy(out=c[:], in_=d[:].indirect(pos2_t[:]))
+            eng = nc.vector if i == 7 else nc.gpsimd
+            eng.tensor_scalar(out=cg[:], in0=c[:], scalar1=neg_ref[:, col], scalar2=gain_t[:, col], op0=ALU.add, op1=ALU.mult)
+            eng.tensor_tensor(out=y[g][:, t, :], in0=cg[:], in1=a[:], op=ALU.mult)
+            nc.sync.dma_start(out=out_v[g, t], in_=y[g][:, t, :])
+            if i in (1, 2):
+                deal(nc.scalar.copy, wb_bf[1], wb_raw[1], 64 * (i - 1), 64 * i, 0)
+            if i == 2:
+                wb_q.append(quantize("wbq1", wb_bf[1]))
+            if i in (4, 5):
+                weave(nc.scalar.copy, 0, 64 * (i - 4), 64 * (i - 3))
+            if i == 6:
+                planes(0)
+        weave(nc.scalar.copy, 1, 0, 40)
+        weave(nc.vector.tensor_copy, 1, 40, 128)
+        planes(1)

@@ -30,8 +30,8 @@ def tile_list_clock_selector_scores_kernel(
         ring = ctx.enter_context(tc.tile_pool(name="ring", bufs=3))
         psum = ctx.enter_context(tc.psum_pool(name="psum", bufs=1))
 
-        def held(name, shape, dtype):
-            return keep.tile(shape, dtype, name=name, align_bytes=64)
+        def held(name, shape, dtype, after=None):
+            return keep.tile(shape, dtype, name=name, tag=after or name, align_bytes=64)
 
         def bank(b, name):
             return psum.tile([P, 512], F32, name=name, tag="bank%d" % b)
@@ -55,7 +55,7 @@ def tile_list_clock_selector_scores_kernel(
         gain_t = held("gain_t", [P, 8], F32)
 
         nc.vector.memset(tab_s[:].bitcast(I32), 0)
-        nc.vector.memset(wa_s[:].bitcast(I32), 0)
+        nc.gpsimd.memset(wa_s[:].bitcast(I32), 0)
 
         def load_words(a):
             nc.sync.dma_start(out=tab_w[a][:], in_=tab_words[a].rearrange("p t i -> p (t i)").bitcast(I32))
@@ -69,17 +69,17 @@ def tile_list_clock_selector_scores_kernel(
         wb_v = wb.rearrange("(p j) c -> p j c", j=4)
 
         nc.sync.dma_start(offs_t[:], offs)
-        nc.sync.dma_start(out=w1_lo[:], in_=w1_v[0])
+        nc.sync.dma_start(out=b1_t[:], in_=b1.rearrange("(p t) -> p t", t=4))
+        load_words(0)
         for q in range(4):
             nc.sync.dma_start(out=tab_s[32 * q : 32 * q + 8, :].bitcast(I32), in_=tab_scales[:, 4 * q : 4 * q + 4, :].bitcast(I32))
-        load_words(0)
+        nc.sync.dma_start(out=w1_lo[:], in_=w1_v[0])
         load_words(1)
-        nc.sync.dma_start(out=b1_t[:], in_=b1.rearrange("(p t) -> p t", t=4))
         for c in range(2):
             nc.sync.dma_start(out=w1_hi[c][:], in_=w1_v[1][:, :, 256 * c : 256 * (c + 1)])
-        for q in range(4):
-            nc.gpsimd.dma_start(out=wa_s[32 * q : 32 * q + 4, :].bitcast(I32), in_=wa_scales[0, 4 * q : 4 * q + 4, :].bitcast(I32))
         nc.sync.dma_start(out=wa_w[:].bitcast(I32), in_=wa_words[0].bitcast(I32))
+        for q in range(4):
+            nc.sync.dma_start(out=wa_s[32 * q : 32 * q + 4, :].bitcast(I32), in_=wa_scales[0, 4 * q : 4 * q + 4, :].bitcast(I32))
         nc.sync.dma_start(out=wb_raw[0][:], in_=wb_v[:, :, 0:512])
         load_rows(steep_t, steep)
         load_rows(share_t, share)
@@ -106,12 +106,16 @@ def tile_list_clock_selector_scores_kernel(
             return codes, scales
 
         w1_bf = [held("w1_bf%d" % a, [P, 2048], BF16) for a in range(2)]
-        v_w = [held("v_w%d" % a, [P, S], U32) for a in range(2)]
-        v_s = held("v_s", [P, S], U8)
+        v_w = [held("v_w0", [P, S], U32)]
 
-        deal(nc.scalar.copy, w1_bf[0], w1_lo, 0, 128, 0)
-        nc.vector.tensor_copy(out=v_s[:], in_=tab_s[:].indirect(offs_t[:]))
+        def scalar_cast(out, in_):
+            nc.scalar.activation(out=out, in_=in_, func=ACT.Copy)
+
         nc.vector.tensor_copy(out=v_w[0][:], in_=tab_w[0][:].bitcast(U32).indirect(offs_t[:]))
+        v_s = held("v_s", [P, S], U8, after="tab_w0")
+        nc.vector.tensor_copy(out=v_s[:], in_=tab_s[:].indirect(offs_t[:]))
+        deal(scalar_cast, w1_bf[0], w1_lo, 0, 104, 0)
+        deal(nc.vector.tensor_copy, w1_bf[0], w1_lo, 104, 128, 0)
         w1_q = [quantize("w1q0", w1_bf[0])]
         h_ps = [bank(b, "h_ps%d" % b) for b in range(8)]
 
@@ -131,47 +135,61 @@ def tile_list_clock_selector_scores_kernel(
 
         for b in range(8):
             first_pass(0, b)
+        v_w.append(held("v_w1", [P, S], U32, after="w1_bf0"))
         nc.vector.tensor_copy(out=v_w[1][:], in_=tab_w[1][:].bitcast(U32).indirect(offs_t[:]))
         deal(nc.scalar.copy, w1_bf[1], w1_hi[0], 0, 64, 0)
-        deal(nc.scalar.copy, w1_bf[1], w1_hi[1], 64, 96, 64)
-        deal(nc.vector.tensor_copy, w1_bf[1], w1_hi[1], 96, 128, 64)
+        deal(nc.scalar.copy, w1_bf[1], w1_hi[1], 64, 100, 64)
+        deal(nc.vector.tensor_copy, w1_bf[1], w1_hi[1], 100, 128, 64)
         w1_q.append(quantize("w1q1", w1_bf[1]))
-        for b in range(8):
+        for b in (0, 4, 1, 5, 2, 3, 6, 7):
             first_pass(1, b)
 
         wa_wd = [held("wa_wd%d" % g, [P, 1024], U8) for g in range(2)]
-        wa_sd = [held("wa_sd%d" % g, [P, 512], U8) for g in range(2)]
-        for g in range(2):
-            nc.gpsimd.tensor_copy(
-                out=wa_wd[g][:].rearrange("p (t m b) -> p t m b", t=4, b=2),
-                in_=wa_w[:, 1024 * g : 1024 * (g + 1)].rearrange("p (m t b) -> p t m b", t=4, b=2),
-            )
-            nc.gpsimd.tensor_copy(
-                out=wa_sd[g][:].rearrange("p (t m) -> p t m", t=4),
-                in_=wa_s[:, 512 * g : 512 * (g + 1)].rearrange("p (m t) -> p t m", t=4),
+        wa_sd = held("wa_sd", [P, N], U8, after="w1_bf1")
+
+        def deal_wa_words(g):
+            nc.scalar.copy(
+                out=wa_wd[g][:].bitcast(U16).rearrange("p (t m) -> p m t", t=4),
+                in_=wa_w[:, 1024 * g : 1024 * (g + 1)].bitcast(U16).rearrange("p (m t) -> p m t", t=4),
             )
 
-        wb_bf = [held("wb_bf%d" % g, [P, 2048], BF16) for g in range(2)]
-        deal(nc.scalar.copy, wb_bf[0], wb_raw[0], 0, 128, 0)
+        nc.vector.tensor_copy(
+            out=wa_sd[:].rearrange("p (g t m) -> p g m t", g=2, t=4), in_=wa_s[:].rearrange("p (g m t) -> p g m t", g=2, t=4)
+        )
+        deal_wa_words(0)
 
         h_bf = [held("h_bf%d" % u, [P, 2048], BF16) for u in range(2)]
+        h_rows = held("h_rows", [P, 4, 256], BF16)
         b1_b = b1_t[:].unsqueeze(1).to_broadcast([P, 128, 4])
         h_q = []
-        for b in range(8):
+        for b in (4, 5):
+            for t in range(4):
+                nc.scalar.activation(
+                    out=h_rows[:, t, 128 * (b - 4) : 128 * (b - 3)], in_=h_ps[b][:, 128 * t : 128 * (t + 1)],
+                    func=ACT.Identity, bias=b1_t[:, t : t + 1],
+                )
+        nc.scalar.copy(
+            out=h_bf[1][:, 0:1024].rearrange("p (c i t) -> p c t i", i=4, t=4),
+            in_=h_rows[:].rearrange("p t (c i) -> p c t i", i=4),
+        )
+        for b in (0, 1, 2, 3, 6, 7):
             nc.vector.tensor_tensor(
                 out=h_bf[b // 4][:, 512 * (b % 4) : 512 * (b % 4 + 1)].rearrange("p (n t) -> p n t", t=4),
                 in0=h_ps[b][:].rearrange("p (t n) -> p n t", t=4),
                 in1=b1_b,
                 op=ALU.add,
             )
-            if b == 4:
+            if b == 6:
                 h_q.append(quantize("hq0", h_bf[0]))
+        wb_bf = [held("wb_bf0", [P, 2048], BF16, after="h_rows")]
+        deal(nc.scalar.copy, wb_bf[0], wb_raw[0], 0, 128, 0)
         neg_ss = held("neg_ss", [P, 8], F32)
         neg_ref = held("neg_ref", [P, 8], F32)
         nc.vector.scalar_tensor_tensor(out=neg_ss[:], in0=steep_t[:], scalar=-1.0, in1=share_t[:], op0=ALU.mult, op1=ALU.mult)
         h_q.append(quantize("hq1", h_bf[1]))
         nc.vector.tensor_scalar(out=neg_ref[:], in0=ref_t[:], scalar1=-1.0, scalar2=None, op0=ALU.mult)
         wb_q = [quantize("wbq0", wb_bf[0])]
+        wb_bf.append(held("wb_bf1", [P, 2048], BF16, after="h_rows"))
 
         top = held("top", [P, 8], F32)
         gate_b = held("gate_b", [P, 8], F32)
@@ -183,39 +201,62 @@ def tile_list_clock_selector_scores_kernel(
             s = y[g][:].rearrange("p t (c i) -> p c t i", i=4)[:, c0:c1]
             copy(out=d, in_=s)
 
-        def planes(g):
-            codes, scales = quantize("yq%d" % g, y_bf[g])
-            nc.sync.dma_start(out=out_1[g].rearrange("p m t -> p (m t)").bitcast(I32), in_=codes[:].bitcast(I32))
-            for q in range(4):
-                queue = nc.scalar if (g == 1 and q % 2 == 1) else nc.sync
-                queue.dma_start(out=out_2[g, 4 * q : 4 * q + 4, :].bitcast(I32), in_=scales[32 * q : 32 * q + 4, :].bitcast(I32))
+        def store_words(g, codes, m0, m1):
+            nc.sync.dma_start(
+                out=out_1[g].rearrange("p m t -> p (m t)").bitcast(I32)[:, m0:m1], in_=codes[:, m0:m1].bitcast(I32)
+            )
 
+        def store_scales(g, scales, queues):
+            for q in range(4):
+                queues[q % 2].dma_start(
+                    out=out_2[g, 4 * q : 4 * q + 4, :].bitcast(I32), in_=scales[32 * q : 32 * q + 4, :].bitcast(I32)
+                )
+
+        e_ps, d_ps, e_t = {}, {}, {}
+
+        def score_product(i, u):
+            g, t = i // 4, i % 4
+            e_ps[i, u] = bank(4 * (i % 2) + u, "e_ps%d_%d" % (i, u))
+            nc.tensor.matmul_mx(
+                out=e_ps[i, u][:], lhsT=wa_wd[g][:, 256 * t : 256 * (t + 1)].bitcast(FP4X4),
+                lhsT_scale=wa_sd[:, 128 * i : 128 * (i + 1)],
+                rhs=h_q[u][0][:].bitcast(FP8X4), rhs_scale=h_q[u][1][:], start=True, stop=True,
+            )
+
+        def delay_product(i, u):
+            g, ts = i // 4, slice(128 * (i % 4), 128 * (i % 4 + 1))
+            d_ps[i, u] = bank(4 * (i % 2) + 2 + u, "d_ps%d_%d" % (i, u))
+            nc.tensor.matmul_mx(
+                out=d_ps[i, u][:], lhsT=wb_q[g][0][:, ts].bitcast(FP8X4), lhsT_scale=wb_q[g][1][:, ts],
+                rhs=h_q[u][0][:].bitcast(FP8X4), rhs_scale=h_q[u][1][:], start=True, stop=True,
+            )
+
+        def add_residual(i, u):
+            if u == 0:
+                e_t[i] = ring.tile([P, S], F32, name="e")
+            js = slice(512 * u, 512 * (u + 1))
+            nc.vector.tensor_tensor(out=e_t[i][:, js], in0=e_ps[i, u][:], in1=res_t[i][:, js], op=ALU.add)
+
+        score_product(0, 0)
+        add_residual(0, 0)
         for i in range(8):
             g, t = i // 4, i % 4
-            ts = slice(128 * t, 128 * (t + 1))
             col = slice(i, i + 1)
-            e_ps = [bank(4 * (i % 2) + u, "e_ps%d_%d" % (i, u)) for u in range(2)]
-            d_ps = [bank(4 * (i % 2) + 2 + u, "d_ps%d_%d" % (i, u)) for u in range(2)]
-            for u in range(2):
-                nc.tensor.matmul_mx(
-                    out=e_ps[u][:], lhsT=wa_wd[g][:, 256 * t : 256 * (t + 1)].bitcast(FP4X4), lhsT_scale=wa_sd[g][:, ts],
-                    rhs=h_q[u][0][:].bitcast(FP8X4), rhs_scale=h_q[u][1][:], start=True, stop=True,
-                )
-            for u in range(2):
-                nc.tensor.matmul_mx(
-                    out=d_ps[u][:], lhsT=wb_q[g][0][:, ts].bitcast(FP8X4), lhsT_scale=wb_q[g][1][:, ts],
-                    rhs=h_q[u][0][:].bitcast(FP8X4), rhs_scale=h_q[u][1][:], start=True, stop=True,
-                )
-            e = ring.tile([P, S], F32, name="e")
+            e = e_t[i]
             d = ring.tile([P, S], F32, name="d")
             a = ring.tile([P, M], F32, name="a")
             c = ring.tile([P, M], F32, name="c")
             cg = ring.tile([P, M], F32, name="cg")
+            score_product(i, 1)
+            if i < 7:
+                score_product(i + 1, 0)
             for u in range(2):
-                js = slice(512 * u, 512 * (u + 1))
-                nc.vector.tensor_tensor(out=e[:, js], in0=e_ps[u][:], in1=res_t[i][:, js], op=ALU.add)
+                delay_product(i, u)
+            add_residual(i, 1)
+            if i < 7:
+                add_residual(i + 1, 0)
             for u in range(2):
-                nc.scalar.copy(out=d[:, 512 * u : 512 * (u + 1)], in_=d_ps[u][:])
+                nc.scalar.copy(out=d[:, 512 * u : 512 * (u + 1)], in_=d_ps[i, u][:])
             nc.vector.tensor_reduce(out=top[:, col], in_=e[:], axis=AXIS.X, op=ALU.max)
             if i == 0:
                 nc.vector.tensor_scalar(out=gate_b[:, col], in0=top[:, col], scalar1=neg_ss[:, col], scalar2=None, op0=ALU.mult)
@@ -225,18 +266,36 @@ def tile_list_clock_selector_scores_kernel(
                 out=a[:], in_=e[:].indirect(pos1_t[:]), func=ACT.Sigmoid, bias=gate_b[:, col], scale=steep_t[:, col]
             )
             nc.vector.tensor_copy(out=c[:], in_=d[:].indirect(pos2_t[:]))
-            eng = nc.vector if i == 7 else nc.gpsimd
-            eng.tensor_scalar(out=cg[:], in0=c[:], scalar1=neg_ref[:, col], scalar2=gain_t[:, col], op0=ALU.add, op1=ALU.mult)
-            eng.tensor_tensor(out=y[g][:, t, :], in0=cg[:], in1=a[:], op=ALU.mult)
+            if i < 7:
+                nc.gpsimd.tensor_scalar(out=cg[:], in0=c[:], scalar1=neg_ref[:, col], scalar2=gain_t[:, col], op0=ALU.add, op1=ALU.mult)
+                nc.gpsimd.tensor_tensor(out=y[g][:, t, :], in0=cg[:], in1=a[:], op=ALU.mult)
+            else:
+                nc.vector.tensor_scalar(out=cg[:], in0=c[:], scalar1=neg_ref[:, col], scalar2=gain_t[:, col], op0=ALU.add, op1=ALU.mult)
+                for ms in (slice(0, 256), slice(256, 512)):
+                    nc.vector.tensor_tensor(out=y[g][:, t, ms], in0=cg[:, ms], in1=a[:, ms], op=ALU.mult)
             nc.sync.dma_start(out=out_v[g, t], in_=y[g][:, t, :])
-            if i in (1, 2):
-                deal(nc.scalar.copy, wb_bf[1], wb_raw[1], 64 * (i - 1), 64 * i, 0)
+            if i == 0:
+                deal_wa_words(1)
+            if i < 3:
+                for m0, m1 in ((0, 20), (20, 42), (42, 64), (64, 86), (86, 108), (108, 128))[2 * i : 2 * i + 2]:
+                    deal(nc.scalar.copy, wb_bf[1], wb_raw[1], m0, m1, 0)
             if i == 2:
                 wb_q.append(quantize("wbq1", wb_bf[1]))
             if i in (4, 5):
-                weave(nc.scalar.copy, 0, 64 * (i - 4), 64 * (i - 3))
+                for c0 in (64 * (i - 4), 64 * (i - 4) + 32):
+                    weave(nc.scalar.copy, 0, c0, c0 + 32)
             if i == 6:
-                planes(0)
-        weave(nc.scalar.copy, 1, 0, 40)
-        weave(nc.vector.tensor_copy, 1, 40, 128)
-        planes(1)
+                codes, scales = quantize("yq0", y_bf[0])
+                store_words(0, codes, 0, 512)
+                store_scales(0, scales, (nc.sync, nc.sync))
+        weave(nc.scalar.copy, 1, 0, 48)
+        weave(nc.vector.tensor_copy, 1, 64, 128)
+        weave(nc.vector.tensor_copy, 1, 48, 64)
+        codes = held("yq1_c", [P, 512], U32)
+        scales = held("yq1_s", [P, 512], U8)
+        for m0 in (256, 0):
+            nc.vector.quantize_mx(
+                out=codes[:, m0 : m0 + 256].bitcast(FP8X4), scales=scales[:, m0 : m0 + 256], in_=y_bf[1][:, 4 * m0 : 4 * m0 + 1024]
+            )
+            store_words(1, codes, m0, m0 + 256)
+        store_scales(1, scales, (nc.scalar, nc.sync))

@@ -160,7 +160,7 @@ def tile_list_clock_selector_scores_kernel(
 
         h_bf = [held("h_bf%d" % u, [P, 2048], BF16) for u in range(2)]
         h_rows = held("h_rows", [P, 4, 256], BF16)
-        b1_b = b1_t[:].unsqueeze(1).to_broadcast([P, 128, 4])
+        b1_b = b1_t[:].unsqueeze(1).unsqueeze(3).to_broadcast([P, 64, 4, 2])
         h_q = []
         for b in (4, 5):
             for t in range(4):
@@ -174,9 +174,9 @@ def tile_list_clock_selector_scores_kernel(
         )
         for b in (0, 1, 2, 3, 6, 7):
             nc.vector.tensor_tensor(
-                out=h_bf[b // 4][:, 512 * (b % 4) : 512 * (b % 4 + 1)].rearrange("p (n t) -> p n t", t=4),
-                in0=h_ps[b][:].rearrange("p (t n) -> p n t", t=4),
-                in1=b1_b,
+                out=h_bf[b // 4][:, 512 * (b % 4) : 512 * (b % 4 + 1)].rearrange("p (c i t) -> p c t i", i=2, t=4),
+                in0=b1_b,
+                in1=h_ps[b][:].rearrange("p (t c i) -> p c t i", t=4, i=2),
                 op=ALU.add,
             )
             if b == 6:
@@ -235,7 +235,7 @@ def tile_list_clock_selector_scores_kernel(
             if u == 0:
                 e_t[i] = ring.tile([P, S], F32, name="e")
             js = slice(512 * u, 512 * (u + 1))
-            nc.vector.tensor_tensor(out=e_t[i][:, js], in0=e_ps[i, u][:], in1=res_t[i][:, js], op=ALU.add)
+            nc.vector.tensor_tensor(out=e_t[i][:, js], in0=res_t[i][:, js], in1=e_ps[i, u][:], op=ALU.add)
 
         score_product(0, 0)
         add_residual(0, 0)
@@ -265,13 +265,19 @@ def tile_list_clock_selector_scores_kernel(
             nc.scalar.activation(
                 out=a[:], in_=e[:].indirect(pos1_t[:]), func=ACT.Sigmoid, bias=gate_b[:, col], scale=steep_t[:, col]
             )
-            nc.vector.tensor_copy(out=c[:], in_=d[:].indirect(pos2_t[:]))
             if i < 7:
+                nc.vector.tensor_copy(out=c[:], in_=d[:].indirect(pos2_t[:]))
                 nc.gpsimd.tensor_scalar(out=cg[:], in0=c[:], scalar1=neg_ref[:, col], scalar2=gain_t[:, col], op0=ALU.add, op1=ALU.mult)
                 nc.gpsimd.tensor_tensor(out=y[g][:, t, :], in0=cg[:], in1=a[:], op=ALU.mult)
             else:
-                nc.vector.tensor_scalar(out=cg[:], in0=c[:], scalar1=neg_ref[:, col], scalar2=gain_t[:, col], op0=ALU.add, op1=ALU.mult)
-                for ms in (slice(0, 256), slice(256, 512)):
+                halves = (slice(0, 256), slice(256, 512))
+                for u, ms in enumerate(halves):
+                    nc.vector.tensor_copy(out=c[:, ms], in_=d[:].indirect(pos2_t[:, 16 * u : 16 * (u + 1)]))
+                for ms in halves:
+                    nc.vector.tensor_scalar(
+                        out=cg[:, ms], in0=c[:, ms], scalar1=neg_ref[:, col], scalar2=gain_t[:, col], op0=ALU.add, op1=ALU.mult
+                    )
+                for ms in halves:
                     nc.vector.tensor_tensor(out=y[g][:, t, ms], in0=cg[:, ms], in1=a[:, ms], op=ALU.mult)
             nc.sync.dma_start(out=out_v[g, t], in_=y[g][:, t, :])
             if i == 0:

@@ -16,7 +16,18 @@ AXIS = mybir.AxisListType
 
 K, H, N, T, S, M = 1024, 512, 1024, 2048, 1024, 512
 P = 128
+BANK = 512
+SETS = N // P
+LAST = SETS - 1
 FLOPS = 2 * K * H * S + 2 * 2 * H * N * S
+
+W1_LO_SCALAR = 100
+W1_HI_SCALAR = 104
+H_SCALAR_BANKS = (4, 5)
+H_VECTOR_BANKS = (0, 1, 2, 3, 6, 7)
+H_BANK_ORDER = (0, 4, 1, 5, 2, 3, 6, 7)
+WB_EDGES = [2 * (64 * k // 6) for k in range(7)]
+Y_LAST_SCALAR = 40
 
 
 def tile_list_clock_selector_scores_kernel(
@@ -34,7 +45,7 @@ def tile_list_clock_selector_scores_kernel(
             return keep.tile(shape, dtype, name=name, tag=after or name, align_bytes=64)
 
         def bank(b, name):
-            return psum.tile([P, 512], F32, name=name, tag="bank%d" % b)
+            return psum.tile([P, BANK], F32, name=name, tag="bank%d" % b)
 
         offs_t = lists.tile([P, S // 16], U16, name="offs_t")
         pos1_t = lists.tile([P, M // 16], U16, name="pos1_t")
@@ -45,14 +56,14 @@ def tile_list_clock_selector_scores_kernel(
         wa_w = held("wa_w", [P, 2 * N], U8)
         wa_s = held("wa_s", [P, N], U8)
         w1_lo = held("w1_lo", [P, 4, H], F32)
-        w1_hi = [held("w1_hi%d" % c, [P, 4, H // 2], F32) for c in range(2)]
+        w1_hi = [held("w1_hi%d" % u, [P, 4, H // 2], F32) for u in range(2)]
         wb_raw = [held("wb_raw%d" % g, [P, 4, 512], F32) for g in range(2)]
-        res_t = [held("res%d" % i, [P, S], F32) for i in range(8)]
+        res_t = [held("res%d" % i, [P, S], F32) for i in range(SETS)]
         b1_t = held("b1_t", [P, 4], F32)
-        steep_t = held("steep_t", [P, 8], F32)
-        share_t = held("share_t", [P, 8], F32)
-        ref_t = held("ref_t", [P, 8], F32)
-        gain_t = held("gain_t", [P, 8], F32)
+        steep_t = held("steep_t", [P, SETS], F32)
+        share_t = held("share_t", [P, SETS], F32)
+        ref_t = held("ref_t", [P, SETS], F32)
+        gain_t = held("gain_t", [P, SETS], F32)
 
         nc.vector.memset(tab_s[:].bitcast(I32), 0)
         nc.gpsimd.memset(wa_s[:].bitcast(I32), 0)
@@ -75,11 +86,11 @@ def tile_list_clock_selector_scores_kernel(
             nc.sync.dma_start(out=tab_s[32 * q : 32 * q + 8, :].bitcast(I32), in_=tab_scales[:, 4 * q : 4 * q + 4, :].bitcast(I32))
         nc.sync.dma_start(out=w1_lo[:], in_=w1_v[0])
         load_words(1)
-        for c in range(2):
-            nc.sync.dma_start(out=w1_hi[c][:], in_=w1_v[1][:, :, 256 * c : 256 * (c + 1)])
-        nc.sync.dma_start(out=wa_w[:].bitcast(I32), in_=wa_words[0].bitcast(I32))
         for q in range(4):
             nc.sync.dma_start(out=wa_s[32 * q : 32 * q + 4, :].bitcast(I32), in_=wa_scales[0, 4 * q : 4 * q + 4, :].bitcast(I32))
+        for u in range(2):
+            nc.sync.dma_start(out=w1_hi[u][:], in_=w1_v[1][:, :, 256 * u : 256 * (u + 1)])
+        nc.sync.dma_start(out=wa_w[:].bitcast(I32), in_=wa_words[0].bitcast(I32))
         nc.sync.dma_start(out=wb_raw[0][:], in_=wb_v[:, :, 0:512])
         load_rows(steep_t, steep)
         load_rows(share_t, share)
@@ -91,13 +102,14 @@ def tile_list_clock_selector_scores_kernel(
         load_rows(gain_t, gain)
         nc.sync.dma_start(out=res_t[2][:], in_=res_v[0, 2])
         nc.sync.dma_start(out=wb_raw[1][:], in_=wb_v[:, :, 512:1024])
-        for i in range(3, 8):
+        for i in range(3, SETS):
             nc.sync.dma_start(out=res_t[i][:], in_=res_v[i // 4, i % 4])
 
         def deal(copy, dst, src, m0, m1, src_m0):
-            d = dst[:].rearrange("p (t m j) -> p m j t", t=4, j=4)[:, m0:m1]
-            s = src[:].rearrange("p j (m t) -> p m j t", t=4)[:, m0 - src_m0 : m1 - src_m0]
-            copy(out=d, in_=s)
+            copy(
+                out=dst[:].rearrange("p (t m j) -> p m j t", t=4, j=4)[:, m0:m1],
+                in_=src[:].rearrange("p j (m t) -> p m j t", t=4)[:, m0 - src_m0 : m1 - src_m0],
+            )
 
         def quantize(name, src):
             codes = held(name + "_c", [P, 512], U32)
@@ -105,28 +117,27 @@ def tile_list_clock_selector_scores_kernel(
             nc.vector.quantize_mx(out=codes[:].bitcast(FP8X4), scales=scales[:], in_=src[:])
             return codes, scales
 
-        w1_bf = [held("w1_bf%d" % a, [P, 2048], BF16) for a in range(2)]
-        v_w = [held("v_w0", [P, S], U32)]
-
         def scalar_cast(out, in_):
             nc.scalar.activation(out=out, in_=in_, func=ACT.Copy)
 
+        w1_bf = [held("w1_bf%d" % a, [P, 2048], BF16) for a in range(2)]
+        v_w = [held("v_w0", [P, S], U32)]
         nc.vector.tensor_copy(out=v_w[0][:], in_=tab_w[0][:].bitcast(U32).indirect(offs_t[:]))
         v_s = held("v_s", [P, S], U8, after="tab_w0")
         nc.vector.tensor_copy(out=v_s[:], in_=tab_s[:].indirect(offs_t[:]))
-        deal(scalar_cast, w1_bf[0], w1_lo, 0, 104, 0)
-        deal(nc.vector.tensor_copy, w1_bf[0], w1_lo, 104, 128, 0)
+        deal(scalar_cast, w1_bf[0], w1_lo, 0, W1_LO_SCALAR, 0)
+        deal(nc.vector.tensor_copy, w1_bf[0], w1_lo, W1_LO_SCALAR, 128, 0)
         w1_q = [quantize("w1q0", w1_bf[0])]
         h_ps = [bank(b, "h_ps%d" % b) for b in range(8)]
 
-        def first_pass(a, b):
+        def first_stage_pass(a, b):
             cols = slice(128 * b, 128 * (b + 1))
             for t in range(4):
-                ts = slice(128 * t, 128 * (t + 1))
+                places = slice(128 * t, 128 * (t + 1))
                 nc.tensor.matmul_mx(
-                    out=h_ps[b][:, ts],
-                    lhsT=w1_q[a][0][:, ts].bitcast(FP8X4),
-                    lhsT_scale=w1_q[a][1][:, ts],
+                    out=h_ps[b][:, places],
+                    lhsT=w1_q[a][0][:, places].bitcast(FP8X4),
+                    lhsT_scale=w1_q[a][1][:, places],
                     rhs=v_w[a][:, cols].bitcast(FP8X4),
                     rhs_scale=v_s[4 * a : P, cols],
                     start=(a == 0 and t == 0),
@@ -134,15 +145,15 @@ def tile_list_clock_selector_scores_kernel(
                 )
 
         for b in range(8):
-            first_pass(0, b)
+            first_stage_pass(0, b)
         v_w.append(held("v_w1", [P, S], U32, after="w1_bf0"))
         nc.vector.tensor_copy(out=v_w[1][:], in_=tab_w[1][:].bitcast(U32).indirect(offs_t[:]))
         deal(nc.scalar.copy, w1_bf[1], w1_hi[0], 0, 64, 0)
-        deal(nc.scalar.copy, w1_bf[1], w1_hi[1], 64, 100, 64)
-        deal(nc.vector.tensor_copy, w1_bf[1], w1_hi[1], 100, 128, 64)
+        deal(nc.scalar.copy, w1_bf[1], w1_hi[1], 64, W1_HI_SCALAR, 64)
+        deal(nc.vector.tensor_copy, w1_bf[1], w1_hi[1], W1_HI_SCALAR, 128, 64)
         w1_q.append(quantize("w1q1", w1_bf[1]))
-        for b in (0, 4, 1, 5, 2, 3, 6, 7):
-            first_pass(1, b)
+        for b in H_BANK_ORDER:
+            first_stage_pass(1, b)
 
         wa_wd = [held("wa_wd%d" % g, [P, 1024], U8) for g in range(2)]
         wa_sd = held("wa_sd", [P, N], U8, after="w1_bf1")
@@ -162,44 +173,47 @@ def tile_list_clock_selector_scores_kernel(
         h_rows = held("h_rows", [P, 4, 256], BF16)
         b1_b = b1_t[:].unsqueeze(1).unsqueeze(3).to_broadcast([P, 64, 4, 2])
         h_q = []
-        for b in (4, 5):
+        for place, b in enumerate(H_SCALAR_BANKS):
             for t in range(4):
                 nc.scalar.activation(
-                    out=h_rows[:, t, 128 * (b - 4) : 128 * (b - 3)], in_=h_ps[b][:, 128 * t : 128 * (t + 1)],
+                    out=h_rows[:, t, 128 * place : 128 * (place + 1)], in_=h_ps[b][:, 128 * t : 128 * (t + 1)],
                     func=ACT.Identity, bias=b1_t[:, t : t + 1],
                 )
         nc.scalar.copy(
             out=h_bf[1][:, 0:1024].rearrange("p (c i t) -> p c t i", i=4, t=4),
             in_=h_rows[:].rearrange("p t (c i) -> p c t i", i=4),
         )
-        for b in (0, 1, 2, 3, 6, 7):
+        for b in H_VECTOR_BANKS:
             nc.vector.tensor_tensor(
                 out=h_bf[b // 4][:, 512 * (b % 4) : 512 * (b % 4 + 1)].rearrange("p (c i t) -> p c t i", i=2, t=4),
                 in0=b1_b,
                 in1=h_ps[b][:].rearrange("p (t c i) -> p c t i", t=4, i=2),
                 op=ALU.add,
             )
-            if b == 6:
+            if b == H_VECTOR_BANKS[4]:
                 h_q.append(quantize("hq0", h_bf[0]))
         wb_bf = [held("wb_bf0", [P, 2048], BF16, after="h_rows")]
         deal(nc.scalar.copy, wb_bf[0], wb_raw[0], 0, 128, 0)
-        neg_ss = held("neg_ss", [P, 8], F32)
-        neg_ref = held("neg_ref", [P, 8], F32)
-        nc.vector.scalar_tensor_tensor(out=neg_ss[:], in0=steep_t[:], scalar=-1.0, in1=share_t[:], op0=ALU.mult, op1=ALU.mult)
+        neg_ss = held("neg_ss", [P, SETS], F32)
+        neg_ref = held("neg_ref", [P, SETS], F32)
+        ss = held("ss", [P, SETS], F32)
+        nc.gpsimd.tensor_tensor(out=ss[:], in0=steep_t[:], in1=share_t[:], op=ALU.mult)
+        nc.gpsimd.tensor_scalar(out=neg_ss[:], in0=ss[:], scalar1=-1.0, scalar2=0.0, op0=ALU.mult, op1=ALU.add)
         h_q.append(quantize("hq1", h_bf[1]))
-        nc.vector.tensor_scalar(out=neg_ref[:], in0=ref_t[:], scalar1=-1.0, scalar2=None, op0=ALU.mult)
+        nc.gpsimd.tensor_scalar(out=neg_ref[:], in0=ref_t[:], scalar1=-1.0, scalar2=0.0, op0=ALU.mult, op1=ALU.add)
         wb_q = [quantize("wbq0", wb_bf[0])]
         wb_bf.append(held("wb_bf1", [P, 2048], BF16, after="h_rows"))
 
-        top = held("top", [P, 8], F32)
-        gate_b = held("gate_b", [P, 8], F32)
+        top = held("top", [P, SETS], F32)
+        gate_b = held("gate_b", [P, SETS], F32)
         y = [held("y%d" % g, [P, 4, M], F32) for g in range(2)]
         y_bf = [held("y_bf%d" % g, [P, 2048], BF16) for g in range(2)]
 
-        def weave(copy, g, c0, c1):
-            d = y_bf[g][:].rearrange("p (c i t) -> p c t i", i=4, t=4)[:, c0:c1]
-            s = y[g][:].rearrange("p t (c i) -> p c t i", i=4)[:, c0:c1]
-            copy(out=d, in_=s)
+        def regroup(copy, g, c0, c1):
+            copy(
+                out=y_bf[g][:].rearrange("p (c i t) -> p c t i", i=4, t=4)[:, c0:c1],
+                in_=y[g][:].rearrange("p t (c i) -> p c t i", i=4)[:, c0:c1],
+            )
 
         def store_words(g, codes, m0, m1):
             nc.sync.dma_start(
@@ -224,84 +238,88 @@ def tile_list_clock_selector_scores_kernel(
             )
 
         def delay_product(i, u):
-            g, ts = i // 4, slice(128 * (i % 4), 128 * (i % 4 + 1))
+            g, places = i // 4, slice(128 * (i % 4), 128 * (i % 4 + 1))
             d_ps[i, u] = bank(4 * (i % 2) + 2 + u, "d_ps%d_%d" % (i, u))
             nc.tensor.matmul_mx(
-                out=d_ps[i, u][:], lhsT=wb_q[g][0][:, ts].bitcast(FP8X4), lhsT_scale=wb_q[g][1][:, ts],
+                out=d_ps[i, u][:], lhsT=wb_q[g][0][:, places].bitcast(FP8X4), lhsT_scale=wb_q[g][1][:, places],
                 rhs=h_q[u][0][:].bitcast(FP8X4), rhs_scale=h_q[u][1][:], start=True, stop=True,
             )
 
         def add_residual(i, u):
             if u == 0:
                 e_t[i] = ring.tile([P, S], F32, name="e")
-            js = slice(512 * u, 512 * (u + 1))
-            nc.vector.tensor_tensor(out=e_t[i][:, js], in0=res_t[i][:, js], in1=e_ps[i, u][:], op=ALU.add)
+            cols = slice(BANK * u, BANK * (u + 1))
+            nc.vector.tensor_tensor(out=e_t[i][:, cols], in0=res_t[i][:, cols], in1=e_ps[i, u][:], op=ALU.add)
 
         score_product(0, 0)
         add_residual(0, 0)
-        for i in range(8):
+        for i in range(SETS):
             g, t = i // 4, i % 4
             col = slice(i, i + 1)
             e = e_t[i]
             d = ring.tile([P, S], F32, name="d")
-            a = ring.tile([P, M], F32, name="a")
-            c = ring.tile([P, M], F32, name="c")
-            cg = ring.tile([P, M], F32, name="cg")
+            gate = ring.tile([P, M], F32, name="gate")
+            picked = ring.tile([P, M], F32, name="picked")
+            level = ring.tile([P, M], F32, name="level")
             score_product(i, 1)
-            if i < 7:
+            if i < LAST:
                 score_product(i + 1, 0)
             for u in range(2):
                 delay_product(i, u)
             add_residual(i, 1)
-            if i < 7:
+            if i < LAST:
                 add_residual(i + 1, 0)
             for u in range(2):
-                nc.scalar.copy(out=d[:, 512 * u : 512 * (u + 1)], in_=d_ps[i, u][:])
+                nc.scalar.copy(out=d[:, BANK * u : BANK * (u + 1)], in_=d_ps[i, u][:])
             nc.vector.tensor_reduce(out=top[:, col], in_=e[:], axis=AXIS.X, op=ALU.max)
             if i == 0:
                 nc.vector.tensor_scalar(out=gate_b[:, col], in0=top[:, col], scalar1=neg_ss[:, col], scalar2=None, op0=ALU.mult)
             else:
                 nc.scalar.activation(out=gate_b[:, col], in_=top[:, col], func=ACT.Identity, scale=neg_ss[:, col])
             nc.scalar.activation(
-                out=a[:], in_=e[:].indirect(pos1_t[:]), func=ACT.Sigmoid, bias=gate_b[:, col], scale=steep_t[:, col]
+                out=gate[:], in_=e[:].indirect(pos1_t[:]), func=ACT.Sigmoid, bias=gate_b[:, col], scale=steep_t[:, col]
             )
-            if i < 7:
-                nc.vector.tensor_copy(out=c[:], in_=d[:].indirect(pos2_t[:]))
-                nc.gpsimd.tensor_scalar(out=cg[:], in0=c[:], scalar1=neg_ref[:, col], scalar2=gain_t[:, col], op0=ALU.add, op1=ALU.mult)
-                nc.gpsimd.tensor_tensor(out=y[g][:, t, :], in0=cg[:], in1=a[:], op=ALU.mult)
+            if i < LAST:
+                nc.vector.tensor_copy(out=picked[:], in_=d[:].indirect(pos2_t[:]))
+                nc.gpsimd.tensor_scalar(
+                    out=level[:], in0=picked[:], scalar1=neg_ref[:, col], scalar2=gain_t[:, col], op0=ALU.add, op1=ALU.mult
+                )
+                nc.gpsimd.tensor_tensor(out=y[g][:, t, :], in0=level[:], in1=gate[:], op=ALU.mult)
             else:
-                halves = (slice(0, 256), slice(256, 512))
-                for u, ms in enumerate(halves):
-                    nc.vector.tensor_copy(out=c[:, ms], in_=d[:].indirect(pos2_t[:, 16 * u : 16 * (u + 1)]))
-                for ms in halves:
+                halves = (slice(0, M // 2), slice(M // 2, M))
+                for u, cols in enumerate(halves):
+                    nc.vector.tensor_copy(out=picked[:, cols], in_=d[:].indirect(pos2_t[:, 16 * u : 16 * (u + 1)]))
+                for cols in halves:
                     nc.vector.tensor_scalar(
-                        out=cg[:, ms], in0=c[:, ms], scalar1=neg_ref[:, col], scalar2=gain_t[:, col], op0=ALU.add, op1=ALU.mult
+                        out=level[:, cols], in0=picked[:, cols], scalar1=neg_ref[:, col], scalar2=gain_t[:, col],
+                        op0=ALU.add, op1=ALU.mult,
                     )
-                for ms in halves:
-                    nc.vector.tensor_tensor(out=y[g][:, t, ms], in0=cg[:, ms], in1=a[:, ms], op=ALU.mult)
+                for cols in halves:
+                    nc.vector.tensor_tensor(out=y[g][:, t, cols], in0=level[:, cols], in1=gate[:, cols], op=ALU.mult)
             nc.sync.dma_start(out=out_v[g, t], in_=y[g][:, t, :])
+
             if i == 0:
                 deal_wa_words(1)
             if i < 3:
-                for m0, m1 in ((0, 20), (20, 42), (42, 64), (64, 86), (86, 108), (108, 128))[2 * i : 2 * i + 2]:
-                    deal(nc.scalar.copy, wb_bf[1], wb_raw[1], m0, m1, 0)
+                for k in (2 * i, 2 * i + 1):
+                    deal(nc.scalar.copy, wb_bf[1], wb_raw[1], WB_EDGES[k], WB_EDGES[k + 1], 0)
             if i == 2:
                 wb_q.append(quantize("wbq1", wb_bf[1]))
             if i in (4, 5):
-                for c0 in (64 * (i - 4), 64 * (i - 4) + 32):
-                    weave(nc.scalar.copy, 0, c0, c0 + 32)
+                for k in (2 * (i - 4), 2 * (i - 4) + 1):
+                    regroup(nc.scalar.copy, 0, 32 * k, 32 * (k + 1))
             if i == 6:
                 codes, scales = quantize("yq0", y_bf[0])
-                store_words(0, codes, 0, 512)
+                store_words(0, codes, 0, M)
                 store_scales(0, scales, (nc.sync, nc.sync))
-        weave(nc.scalar.copy, 1, 0, 48)
-        weave(nc.vector.tensor_copy, 1, 64, 128)
-        weave(nc.vector.tensor_copy, 1, 48, 64)
-        codes = held("yq1_c", [P, 512], U32)
-        scales = held("yq1_s", [P, 512], U8)
-        for m0 in (256, 0):
-            nc.vector.quantize_mx(
-                out=codes[:, m0 : m0 + 256].bitcast(FP8X4), scales=scales[:, m0 : m0 + 256], in_=y_bf[1][:, 4 * m0 : 4 * m0 + 1024]
-            )
-            store_words(1, codes, m0, m0 + 256)
+
+        regroup(nc.scalar.copy, 1, 0, Y_LAST_SCALAR)
+        regroup(nc.vector.tensor_copy, 1, 64, 128)
+        regroup(nc.vector.tensor_copy, 1, Y_LAST_SCALAR, 64)
+        codes = held("yq1_c", [P, M], U32)
+        scales = held("yq1_s", [P, M], U8)
+        for m0 in (M // 2, 0):
+            m1 = m0 + M // 2
+            nc.vector.quantize_mx(out=codes[:, m0:m1].bitcast(FP8X4), scales=scales[:, m0:m1], in_=y_bf[1][:, 4 * m0 : 4 * m1])
+            store_words(1, codes, m0, m1)
         store_scales(1, scales, (nc.scalar, nc.sync))

from contextlib import ExitStack

import concourse.mybir as mybir

F32 = mybir.dt.float32
BF16 = mybir.dt.bfloat16
I32 = mybir.dt.int32
U32 = mybir.dt.uint32
U16 = mybir.dt.uint16
U8 = mybir.dt.uint8
FP8X4 = mybir.dt.float8_e4m3fn_x4
FP4X4 = mybir.dt.float4_e2m1fn_x4
ALU = mybir.AluOpType
ACT = mybir.ActivationFunctionType
AXIS = mybir.AxisListType

K, H, N, T, S, M = 1024, 512, 1024, 2048, 1024, 512
P = 128
BANK = 512
SETS = N // P
LAST = SETS - 1
FLOPS = 2 * K * H * S + 2 * 2 * H * N * S

W1_LO_SCALAR = 100
W1_HI_SCALAR = 104
H_SCALAR_BANKS = (4, 5)
H_VECTOR_BANKS = (0, 1, 2, 3, 6, 7)
H_BANK_ORDER = (0, 4, 1, 5, 2, 3, 6, 7)
WB_EDGES = [2 * (64 * k // 6) for k in range(7)]
Y_LAST_SCALAR = 40


def tile_list_clock_selector_scores_kernel(
    tc, tab_words, tab_scales, offs, pos1, pos2, w1, b1, wa_words, wa_scales, res, wb, steep, share, ref, gain,
    out_0, out_1, out_2,
):
    nc = tc.nc
    with ExitStack() as ctx:
        lists = ctx.enter_context(tc.tile_pool(name="lists", bufs=1))
        keep = ctx.enter_context(tc.tile_pool(name="keep", bufs=1))
        ring = ctx.enter_context(tc.tile_pool(name="ring", bufs=3))
        psum = ctx.enter_context(tc.psum_pool(name="psum", bufs=1))

        def held(name, shape, dtype, after=None):
            return keep.tile(shape, dtype, name=name, tag=after or name, align_bytes=64)

        def bank(b, name):
            return psum.tile([P, BANK], F32, name=name, tag="bank%d" % b)

        offs_t = lists.tile([P, S // 16], U16, name="offs_t")
        pos1_t = lists.tile([P, M // 16], U16, name="pos1_t")
        pos2_t = lists.tile([P, M // 16], U16, name="pos2_t")

        tab_w = [held("tab_w%d" % a, [P, T], I32) for a in range(2)]
        tab_s = held("tab_s", [P, T], U8)
        wa_w = held("wa_w", [P, 2 * N], U8)
        wa_s = held("wa_s", [P, N], U8)
        w1_lo = held("w1_lo", [P, 4, H], F32)
        w1_hi = [held("w1_hi%d" % u, [P, 4, H // 2], F32) for u in range(2)]
        wb_raw = [held("wb_raw%d" % g, [P, 4, 512], F32) for g in range(2)]
        res_t = [held("res%d" % i, [P, S], F32) for i in range(SETS)]
        b1_t = held("b1_t", [P, 4], F32)
        steep_t = held("steep_t", [P, SETS], F32)
        share_t = held("share_t", [P, SETS], F32)
        ref_t = held("ref_t", [P, SETS], F32)
        gain_t = held("gain_t", [P, SETS], F32)

        nc.vector.memset(tab_s[:].bitcast(I32), 0)
        nc.gpsimd.memset(wa_s[:].bitcast(I32), 0)

        def load_words(a):
            nc.sync.dma_start(out=tab_w[a][:], in_=tab_words[a].rearrange("p t i -> p (t i)").bitcast(I32))

        def load_rows(tile, vec):
            nc.sync.dma_start(out=tile[:].rearrange("p (g t) -> p g t", t=4), in_=vec.rearrange("(g p t) -> p g t", g=2, t=4))

        res_v = res.rearrange("(g p t) j -> g t p j", g=2, t=4)
        out_v = out_0.rearrange("(g p t) m -> g t p m", g=2, t=4)
        w1_v = w1.rearrange("(a p j) c -> a p j c", a=2, j=4)
        wb_v = wb.rearrange("(p j) c -> p j c", j=4)

        nc.sync.dma_start(offs_t[:], offs)
        nc.sync.dma_start(out=b1_t[:], in_=b1.rearrange("(p t) -> p t", t=4))
        load_words(0)
        for q in range(4):
            nc.sync.dma_start(out=tab_s[32 * q : 32 * q + 8, :].bitcast(I32), in_=tab_scales[:, 4 * q : 4 * q + 4, :].bitcast(I32))
        nc.sync.dma_start(out=w1_lo[:], in_=w1_v[0])
        load_words(1)
        for q in range(4):
            nc.sync.dma_start(out=wa_s[32 * q : 32 * q + 4, :].bitcast(I32), in_=wa_scales[0, 4 * q : 4 * q + 4, :].bitcast(I32))
        for u in range(2):
            nc.sync.dma_start(out=w1_hi[u][:], in_=w1_v[1][:, :, 256 * u : 256 * (u + 1)])
        nc.sync.dma_start(out=wa_w[:].bitcast(I32), in_=wa_words[0].bitcast(I32))
        nc.sync.dma_start(out=wb_raw[0][:], in_=wb_v[:, :, 0:512])
        load_rows(steep_t, steep)
        load_rows(share_t, share)
        nc.sync.dma_start(out=res_t[0][:], in_=res_v[0, 0])
        nc.sync.dma_start(pos1_t[:], pos1)
        nc.sync.dma_start(pos2_t[:], pos2)
        nc.sync.dma_start(out=res_t[1][:], in_=res_v[0, 1])
        load_rows(ref_t, ref)
        load_rows(gain_t, gain)
        nc.sync.dma_start(out=res_t[2][:], in_=res_v[0, 2])
        nc.sync.dma_start(out=wb_raw[1][:], in_=wb_v[:, :, 512:1024])
        for i in range(3, SETS):
            nc.sync.dma_start(out=res_t[i][:], in_=res_v[i // 4, i % 4])

        def deal(copy, dst, src, m0, m1, src_m0):
            copy(
                out=dst[:].rearrange("p (t m j) -> p m j t", t=4, j=4)[:, m0:m1],
                in_=src[:].rearrange("p j (m t) -> p m j t", t=4)[:, m0 - src_m0 : m1 - src_m0],
            )

        def quantize(name, src):
            codes = held(name + "_c", [P, 512], U32)
            scales = held(name + "_s", [P, 512], U8)
            nc.vector.quantize_mx(out=codes[:].bitcast(FP8X4), scales=scales[:], in_=src[:])
            return codes, scales

        def scalar_cast(out, in_):
            nc.scalar.activation(out=out, in_=in_, func=ACT.Copy)

        w1_bf = [held("w1_bf%d" % a, [P, 2048], BF16) for a in range(2)]
        v_w = [held("v_w0", [P, S], U32)]
        nc.vector.tensor_copy(out=v_w[0][:], in_=tab_w[0][:].bitcast(U32).indirect(offs_t[:]))
        v_s = held("v_s", [P, S], U8, after="tab_w0")
        nc.vector.tensor_copy(out=v_s[:], in_=tab_s[:].indirect(offs_t[:]))
        deal(scalar_cast, w1_bf[0], w1_lo, 0, W1_LO_SCALAR, 0)
        deal(nc.vector.tensor_copy, w1_bf[0], w1_lo, W1_LO_SCALAR, 128, 0)
        w1_q = [quantize("w1q0", w1_bf[0])]
        h_ps = [bank(b, "h_ps%d" % b) for b in range(8)]

        def first_stage_pass(a, b):
            cols = slice(128 * b, 128 * (b + 1))
            for t in range(4):
                places = slice(128 * t, 128 * (t + 1))
                nc.tensor.matmul_mx(
                    out=h_ps[b][:, places],
                    lhsT=w1_q[a][0][:, places].bitcast(FP8X4),
                    lhsT_scale=w1_q[a][1][:, places],
                    rhs=v_w[a][:, cols].bitcast(FP8X4),
                    rhs_scale=v_s[4 * a : P, cols],
                    start=(a == 0 and t == 0),
                    stop=(a == 1 and t == 3),
                )

        for b in range(8):
            first_stage_pass(0, b)
        v_w.append(held("v_w1", [P, S], U32, after="w1_bf0"))
        nc.vector.tensor_copy(out=v_w[1][:], in_=tab_w[1][:].bitcast(U32).indirect(offs_t[:]))
        deal(nc.scalar.copy, w1_bf[1], w1_hi[0], 0, 64, 0)
        deal(nc.scalar.copy, w1_bf[1], w1_hi[1], 64, W1_HI_SCALAR, 64)
        deal(nc.vector.tensor_copy, w1_bf[1], w1_hi[1], W1_HI_SCALAR, 128, 64)
        w1_q.append(quantize("w1q1", w1_bf[1]))
        for b in H_BANK_ORDER:
            first_stage_pass(1, b)

        wa_wd = [held("wa_wd%d" % g, [P, 1024], U8) for g in range(2)]
        wa_sd = held("wa_sd", [P, N], U8, after="w1_bf1")

        def deal_wa_words(g):
            nc.scalar.copy(
                out=wa_wd[g][:].bitcast(U16).rearrange("p (t m) -> p m t", t=4),
                in_=wa_w[:, 1024 * g : 1024 * (g + 1)].bitcast(U16).rearrange("p (m t) -> p m t", t=4),
            )

        nc.vector.tensor_copy(
            out=wa_sd[:].rearrange("p (g t m) -> p g m t", g=2, t=4), in_=wa_s[:].rearrange("p (g m t) -> p g m t", g=2, t=4)
        )
        deal_wa_words(0)

        h_bf = [held("h_bf%d" % u, [P, 2048], BF16) for u in range(2)]
        h_rows = held("h_rows", [P, 4, 256], BF16)
        b1_b = b1_t[:].unsqueeze(1).unsqueeze(3).to_broadcast([P, 64, 4, 2])
        h_q = []
        for place, b in enumerate(H_SCALAR_BANKS):
            for t in range(4):
                nc.scalar.activation(
                    out=h_rows[:, t, 128 * place : 128 * (place + 1)], in_=h_ps[b][:, 128 * t : 128 * (t + 1)],
                    func=ACT.Identity, bias=b1_t[:, t : t + 1],
                )
        nc.scalar.copy(
            out=h_bf[1][:, 0:1024].rearrange("p (c i t) -> p c t i", i=4, t=4),
            in_=h_rows[:].rearrange("p t (c i) -> p c t i", i=4),
        )
        for b in H_VECTOR_BANKS:
            nc.vector.tensor_tensor(
                out=h_bf[b // 4][:, 512 * (b % 4) : 512 * (b % 4 + 1)].rearrange("p (c i t) -> p c t i", i=2, t=4),
                in0=b1_b,
                in1=h_ps[b][:].rearrange("p (t c i) -> p c t i", t=4, i=2),
                op=ALU.add,
            )
            if b == H_VECTOR_BANKS[4]:
                h_q.append(quantize("hq0", h_bf[0]))
        wb_bf = [held("wb_bf0", [P, 2048], BF16, after="h_rows")]
        deal(nc.scalar.copy, wb_bf[0], wb_raw[0], 0, 128, 0)
        neg_ss = held("neg_ss", [P, SETS], F32)
        neg_ref = held("neg_ref", [P, SETS], F32)
        ss = held("ss", [P, SETS], F32)
        nc.gpsimd.tensor_tensor(out=ss[:], in0=steep_t[:], in1=share_t[:], op=ALU.mult)
        nc.gpsimd.tensor_scalar(out=neg_ss[:], in0=ss[:], scalar1=-1.0, scalar2=0.0, op0=ALU.mult, op1=ALU.add)
        h_q.append(quantize("hq1", h_bf[1]))
        nc.gpsimd.tensor_scalar(out=neg_ref[:], in0=ref_t[:], scalar1=-1.0, scalar2=0.0, op0=ALU.mult, op1=ALU.add)
        wb_q = [quantize("wbq0", wb_bf[0])]
        wb_bf.append(held("wb_bf1", [P, 2048], BF16, after="h_rows"))

        top = held("top", [P, SETS], F32)
        gate_b = held("gate_b", [P, SETS], F32)
        y = [held("y%d" % g, [P, 4, M], F32) for g in range(2)]
        y_bf = [held("y_bf%d" % g, [P, 2048], BF16) for g in range(2)]

        def regroup(copy, g, c0, c1):
            copy(
                out=y_bf[g][:].rearrange("p (c i t) -> p c t i", i=4, t=4)[:, c0:c1],
                in_=y[g][:].rearrange("p t (c i) -> p c t i", i=4)[:, c0:c1],
            )

        def store_words(g, codes, m0, m1):
            nc.sync.dma_start(
                out=out_1[g].rearrange("p m t -> p (m t)").bitcast(I32)[:, m0:m1], in_=codes[:, m0:m1].bitcast(I32)
            )

        def store_scales(g, scales, queues):
            for q in range(4):
                queues[q % 2].dma_start(
                    out=out_2[g, 4 * q : 4 * q + 4, :].bitcast(I32), in_=scales[32 * q : 32 * q + 4, :].bitcast(I32)
                )

        e_ps, d_ps, e_t = {}, {}, {}

        def score_product(i, u):
            g, t = i // 4, i % 4
            e_ps[i, u] = bank(4 * (i % 2) + u, "e_ps%d_%d" % (i, u))
            nc.tensor.matmul_mx(
                out=e_ps[i, u][:], lhsT=wa_wd[g][:, 256 * t : 256 * (t + 1)].bitcast(FP4X4),
                lhsT_scale=wa_sd[:, 128 * i : 128 * (i + 1)],
                rhs=h_q[u][0][:].bitcast(FP8X4), rhs_scale=h_q[u][1][:], start=True, stop=True,
            )

        def delay_product(i, u):
            g, places = i // 4, slice(128 * (i % 4), 128 * (i % 4 + 1))
            d_ps[i, u] = bank(4 * (i % 2) + 2 + u, "d_ps%d_%d" % (i, u))
            nc.tensor.matmul_mx(
                out=d_ps[i, u][:], lhsT=wb_q[g][0][:, places].bitcast(FP8X4), lhsT_scale=wb_q[g][1][:, places],
                rhs=h_q[u][0][:].bitcast(FP8X4), rhs_scale=h_q[u][1][:], start=True, stop=True,
            )

        def add_residual(i, u):
            if u == 0:
                e_t[i] = ring.tile([P, S], F32, name="e")
            cols = slice(BANK * u, BANK * (u + 1))
            nc.vector.tensor_tensor(out=e_t[i][:, cols], in0=res_t[i][:, cols], in1=e_ps[i, u][:], op=ALU.add)

        score_product(0, 0)
        add_residual(0, 0)
        for i in range(SETS):
            g, t = i // 4, i % 4
            col = slice(i, i + 1)
            e = e_t[i]
            d = ring.tile([P, S], F32, name="d")
            gate = ring.tile([P, M], F32, name="gate")
            picked = ring.tile([P, M], F32, name="picked")
            level = ring.tile([P, M], F32, name="level")
            score_product(i, 1)
            if i < LAST:
                score_product(i + 1, 0)
            for u in range(2):
                delay_product(i, u)
            add_residual(i, 1)
            if i < LAST:
                add_residual(i + 1, 0)
            for u in range(2):
                nc.scalar.copy(out=d[:, BANK * u : BANK * (u + 1)], in_=d_ps[i, u][:])
            nc.vector.tensor_reduce(out=top[:, col], in_=e[:], axis=AXIS.X, op=ALU.max)
            if i == 0:
                nc.vector.tensor_scalar(out=gate_b[:, col], in0=top[:, col], scalar1=neg_ss[:, col], scalar2=None, op0=ALU.mult)
            else:
                nc.scalar.activation(out=gate_b[:, col], in_=top[:, col], func=ACT.Identity, scale=neg_ss[:, col])
            nc.scalar.activation(
                out=gate[:], in_=e[:].indirect(pos1_t[:]), func=ACT.Sigmoid, bias=gate_b[:, col], scale=steep_t[:, col]
            )
            if i < LAST:
                nc.vector.tensor_copy(out=picked[:], in_=d[:].indirect(pos2_t[:]))
                nc.gpsimd.tensor_scalar(
                    out=level[:], in0=picked[:], scalar1=neg_ref[:, col], scalar2=gain_t[:, col], op0=ALU.add, op1=ALU.mult
                )
                nc.gpsimd.tensor_tensor(out=y[g][:, t, :], in0=level[:], in1=gate[:], op=ALU.mult)
            else:
                halves = (slice(0, M // 2), slice(M // 2, M))
                for u, cols in enumerate(halves):
                    nc.vector.tensor_copy(out=picked[:, cols], in_=d[:].indirect(pos2_t[:, 16 * u : 16 * (u + 1)]))
                for cols in halves:
                    nc.vector.tensor_scalar(
                        out=level[:, cols], in0=picked[:, cols], scalar1=neg_ref[:, col], scalar2=gain_t[:, col],
                        op0=ALU.add, op1=ALU.mult,
                    )
                for cols in halves:
                    nc.vector.tensor_tensor(out=y[g][:, t, cols], in0=level[:, cols], in1=gate[:, cols], op=ALU.mult)
            nc.sync.dma_start(out=out_v[g, t], in_=y[g][:, t, :])

            if i == 0:
                deal_wa_words(1)
            if i < 3:
                for k in (2 * i, 2 * i + 1):
                    deal(nc.scalar.copy, wb_bf[1], wb_raw[1], WB_EDGES[k], WB_EDGES[k + 1], 0)
            if i == 2:
                wb_q.append(quantize("wbq1", wb_bf[1]))
            if i in (4, 5):
                for k in (2 * (i - 4), 2 * (i - 4) + 1):
                    regroup(nc.scalar.copy, 0, 32 * k, 32 * (k + 1))
            if i == 6:
                codes, scales = quantize("yq0", y_bf[0])
                store_words(0, codes, 0, M)
                store_scales(0, scales, (nc.sync, nc.sync))

        regroup(nc.scalar.copy, 1, 0, Y_LAST_SCALAR)
        regroup(nc.vector.tensor_copy, 1, 64, 128)
        regroup(nc.vector.tensor_copy, 1, Y_LAST_SCALAR, 64)
        codes = held("yq1_c", [P, M], U32)
        scales = held("yq1_s", [P, M], U8)
        for m0 in (M // 2, 0):
            m1 = m0 + M // 2
            nc.vector.quantize_mx(out=codes[:, m0:m1].bitcast(FP8X4), scales=scales[:, m0:m1], in_=y_bf[1][:, 4 * m0 : 4 * m1])
            store_words(1, codes, m0, m1)
        store_scales(1, scales, (nc.scalar, nc.sync))
